import numpy as np
import ml_dtypes


def mxq(x, axis, fmt="e4m3"):
    dtype, down = {"e4m3": (ml_dtypes.float8_e4m3fn, 7), "e5m2": (ml_dtypes.float8_e5m2, 14)}[fmt]
    v = np.moveaxis(np.asarray(x, np.float32).astype(ml_dtypes.bfloat16).astype(np.float64), axis, -1)
    blocks = v.reshape(v.shape[:-1] + (-1, 32))
    amax = np.abs(blocks).max(-1, keepdims=True)
    byte = np.maximum(np.where(amax > 0, np.frexp(amax)[1] - 1 + 127, 0) - down, 1)
    scale = np.exp2(byte - 127.0)
    codes = (blocks / scale).astype(np.float32).astype(dtype).astype(np.float64)
    return np.moveaxis((codes * scale).reshape(v.shape), -1, axis)


WIDE = False


def mx_kscale(k):
    if not WIDE:
        return np.ones(k)
    levels = np.array([10, -10, 5, -5, 0])
    if k % 512:
        return np.exp2(np.random.permutation(np.resize(levels, k // 32))).repeat(32)
    a = np.empty((k // 512, 16))
    for p in range(k // 512):
        a[p, :8] = np.random.permutation(np.resize(levels, 8))
        for g in range(8):
            far = levels[np.abs(levels - a[p, g]) >= 10]
            a[p, g + 8] = far[np.random.randint(len(far))]
    return np.exp2(a.ravel()).repeat(32)


def f64(x):
    return np.asarray(x).astype(np.float64)


def striped(idx):
    return np.tile(idx.reshape(-1, 16).T, (8, 1)).astype(np.uint16)


def unstriped(offs):
    return offs[:16].T.reshape(-1).astype(np.int64)


def striped8(idx):
    return np.concatenate([x.reshape(-1, 16).T for x in idx]).astype(np.uint16)


def runs(offs, k):
    lists = np.stack([offs[16 * r : 16 * r + 16].T.reshape(-1) for r in range(8)]).astype(np.int64)
    return lists[np.arange(k) % 512 // 64]


def pack_weight(w):
    k, n = w.shape
    w = f64(np.asarray(w, np.float32).astype(ml_dtypes.bfloat16)).reshape(k // 32, 32, n)
    amax = np.abs(w).max(1)
    byte = np.clip(np.where(amax > 0, np.frexp(amax)[1] - 1 + 127 - 7, 1), 1, 254)
    scaled = (w * np.exp2(127.0 - byte)[:, None, :]).reshape(k, n).astype(np.float32)
    words = np.ascontiguousarray(scaled.reshape(k // 512, 128, 4, n).transpose(0, 1, 3, 2)).astype(ml_dtypes.float8_e4m3fn).view(np.uint8)
    return words, np.ascontiguousarray(byte.astype(np.uint8).reshape(k // 512, 16, n))


def unpack_weight(words, scales):
    g, p, n, _ = words.shape
    vals = np.ascontiguousarray(words).view(ml_dtypes.float8_e4m3fn).astype(np.float64) * np.repeat(np.exp2(scales.astype(np.float64) - 127.0), 8, axis=1)[..., None]
    return vals.transpose(0, 1, 3, 2).reshape(g * 512, n)

def planes(y):
    n, m = y.shape
    v = y.astype(np.float32).astype(ml_dtypes.bfloat16).astype(np.float64).reshape(n // 32, 32, m)
    top = np.abs(v).max(1)
    byte = np.clip(np.where(top > 0, np.frexp(top)[1] - 1 + 127 - 7, 1), 1, 254)
    codes = (v * np.exp2(127.0 - byte)[:, None, :]).reshape(n, m).astype(np.float32).astype(ml_dtypes.float8_e4m3fn).view(np.uint8)
    words = codes.reshape(n // 512, 128, 4, m).transpose(0, 1, 3, 2)
    return np.ascontiguousarray(words), np.ascontiguousarray(byte.astype(np.uint8).reshape(n // 512, 16, m))


K, T, S, N, H, U = 512, 2048, 512, 512, 512, 512


def setup_inputs():
    n = np.random.standard_normal
    s = mx_kscale(K)[:, None]
    u = mx_kscale(H)
    packed_xT = pack_weight(n((K, T)) * s)
    packed_w2 = pack_weight(n((K, H)) / np.sqrt(K) / s)
    packed_w3 = pack_weight(n((H, N)) / np.sqrt(H) / u[:, None])
    return {
        "x_words": packed_xT[0],
        "x_scales": packed_xT[1],
        "w1": (n((K, H)) / np.sqrt(K) / s * u).astype(np.float32),
        "w2_words": packed_w2[0],
        "w2_scales": packed_w2[1],
        "noise": np.random.uniform(0.1, 0.6, (H, U)).astype(np.float32),
        "w3_words": packed_w3[0],
        "w3_scales": packed_w3[1],
        "offs": striped(np.random.permutation(T)[:S]),
        "pr": striped8(np.random.randint(0, U, (8, S))),
    }


def reference(x_words, x_scales, w1, w2_words, w2_scales, noise, w3_words, w3_scales, offs, pr):
    xq = unpack_weight(x_words, x_scales)[:, unstriped(offs)]
    re = mxq(f64(w1), 0, "e4m3").T @ xq
    im = unpack_weight(w2_words, w2_scales).T @ xq
    mg = np.sqrt((im) ** 2 + 0.25)
    ga = np.maximum(mg - (f64(noise)[np.arange(H)[:, None], runs(pr, H)]), 0.25 * mg)
    z = re * (ga / mg)
    out_0 = unpack_weight(w3_words, w3_scales).T @ mxq(z, 0, "e4m3")
    return (out_0,) + planes(out_0)

@@ -1,0 +1,200 @@
+from contextlib import ExitStack
+
+import concourse.mybir as mybir
+
+K, T, S, H, U, N = 512, 2048, 512, 512, 512, 512
+FLOPS = 2 * (2 * K * H * S + H * N * S)
+
+F32 = mybir.dt.float32
+BF16 = mybir.dt.bfloat16
+I32 = mybir.dt.int32
+U32 = mybir.dt.uint32
+U16 = mybir.dt.uint16
+U8 = mybir.dt.uint8
+FP8X4 = mybir.dt.float8_e4m3fn_x4
+ALU = mybir.AluOpType
+ACT = mybir.ActivationFunctionType
+
+P = 128
+PACK = 4
+HALF = 256
+CHUNKS = (128,128,128,128)
+LIST_ROWS = 16
+W1_SPLIT = 256
+
+
+def words_of(dram):
+    return dram[0].rearrange("p n t -> p (n t)").bitcast(I32)
+
+
+def load_scale_rows(queue, tile, dram):
+    for q in range(4):
+        queue.dma_start(out=tile[32 * q : 32 * q + 4, :].bitcast(I32), in_=dram[0, 4 * q : 4 * q + 4, :].bitcast(I32))
+
+
+def deal(nc, dst, src):
+    nc.vector.tensor_copy(out=dst.rearrange("p (t m) -> p m t", t=PACK), in_=src.rearrange("p (m t) -> p m t", t=PACK))
+
+
+def tile_picked_specsub_none_po_kernel(
+    tc, x_words, x_scales, w1, w2_words, w2_scales, noise, w3_words, w3_scales, offs, pr, out_0, out_1, out_2
+):
+    nc = tc.nc
+    halves = S // HALF
+    with ExitStack() as ctx:
+        lists = ctx.enter_context(tc.tile_pool(name="lists", bufs=1))
+        keep = ctx.enter_context(tc.tile_pool(name="keep", bufs=1))
+        psum_a = ctx.enter_context(tc.psum_pool(name="psum_a", bufs=4))
+        psum_b = ctx.enter_context(tc.psum_pool(name="psum_b", bufs=4))
+
+        def sb(shape, dtype, name):
+            return keep.tile(shape, dtype, name=name, align_bytes=64)
+
+        offs_sb = lists.tile([P, S // LIST_ROWS], U16, name="offs_sb")
+        pr_sb = lists.tile([P, S // LIST_ROWS], U16, name="pr_sb")
+        x_all = sb([P, T], U32, "x_all")
+        xs_all = sb([P, T], U8, "xs_all")
+        w2_raw = sb([P, H], I32, "w2_raw")
+        w3_raw = sb([P, N], I32, "w3_raw")
+        w2s_raw = sb([P, H], U8, "w2s_raw")
+        w3s_raw = sb([P, N], U8, "w3s_raw")
+        w1_raw = [sb([P, PACK, W1_SPLIT], F32, "w1a"), sb([P, PACK, H - W1_SPLIT], F32, "w1b")]
+        noise_sb = [sb([P, U], F32, "noise%d" % t) for t in range(PACK)]
+        quarter = sb([P, 1], F32, "quarter")
+        one = sb([P, 1], F32, "one")
+        warm = sb([P, 1], F32, "warm")
+
+        nc.vector.memset(xs_all[:, 0 : T // 2].bitcast(I32), 0)
+        nc.gpsimd.memset(xs_all[:, T // 2 : T].bitcast(I32), 0)
+        nc.vector.memset(w2s_raw[:].bitcast(I32), 0)
+        nc.vector.memset(w3s_raw[:].bitcast(I32), 0)
+        nc.gpsimd.memset(quarter[:], 0.25)
+        nc.gpsimd.memset(one[:], 1.0)
+        nc.scalar.activation(out=warm[:], in_=quarter[:], func=ACT.Abs_reciprocal_sqrt)
+
+        noise_rows = noise.rearrange("(p t) u -> p t u", t=PACK)
+        w1_rows = w1.rearrange("(p j) c -> p j c", j=PACK)
+        nc.sync.dma_start(out=offs_sb[:], in_=offs)
+        nc.sync.dma_start(out=w2_raw[:], in_=words_of(w2_words))
+        load_scale_rows(nc.sync, xs_all, x_scales)
+        nc.sync.dma_start(out=x_all[:].bitcast(I32), in_=words_of(x_words))
+        load_scale_rows(nc.sync, w2s_raw, w2_scales)
+        nc.sync.dma_start(out=w1_raw[0][:], in_=w1_rows[:, :, 0:W1_SPLIT])
+        nc.sync.dma_start(out=w1_raw[1][:], in_=w1_rows[:, :, W1_SPLIT:H])
+        nc.sync.dma_start(out=w3_raw[:], in_=words_of(w3_words))
+        nc.sync.dma_start(out=pr_sb[:], in_=pr)
+        load_scale_rows(nc.sync, w3s_raw, w3_scales)
+        for t in range(PACK):
+            nc.sync.dma_start(out=noise_sb[t][:], in_=noise_rows[:, t, :])
+
+        cols = HALF // LIST_ROWS
+        xq_s = sb([P, S], U8, "xq_s")
+        xq = [sb([P, HALF], U32, "xq0"), sb([P, HALF], U32, "w2s_raw")]
+        w2 = sb([P, H], I32, "w2")
+        w2s = sb([P, H], U8, "w2s")
+        nc.vector.tensor_copy(out=xq_s[:], in_=xs_all[:].indirect(offs_sb[:]))
+        deal(nc, w2[:], w2_raw[:])
+        nc.vector.tensor_copy(out=xq[0][:], in_=x_all[:].indirect(offs_sb[:, 0:cols]))
+        deal(nc, w2s[:], w2s_raw[:])
+        nc.vector.tensor_copy(out=xq[1][:], in_=x_all[:].indirect(offs_sb[:, cols : 2 * cols]))
+
+        def product(out, w, ws, t, rhs, rhs_scale):
+            nc.tensor.matmul_mx(
+                out=out,
+                lhsT=w[:, t * P : (t + 1) * P].bitcast(FP8X4),
+                lhsT_scale=ws[:, t * P : (t + 1) * P],
+                rhs=rhs.bitcast(FP8X4),
+                rhs_scale=rhs_scale,
+                start=True,
+                stop=True,
+            )
+
+        w1_bf = sb([P, H, PACK], BF16, "w1_bf")
+        w1_dealt = w1_bf[:].rearrange("p (t m) j -> p m j t", t=PACK)
+        nc.scalar.copy(out=w1_dealt[:, 0 : W1_SPLIT // PACK], in_=w1_raw[0][:].rearrange("p j (m t) -> p m j t", t=PACK))
+        nc.vector.tensor_copy(out=w1_dealt[:, W1_SPLIT // PACK :], in_=w1_raw[1][:].rearrange("p j (m t) -> p m j t", t=PACK))
+        squares = [sb([P, PACK, HALF], F32, "w1a"), sb([P, PACK, HALF], F32, "w1b")]
+
+        inv_mg = {}
+        for h in range(halves):
+            for pair in range(PACK // 2):
+                im = psum_a.tile([P, 2, HALF], F32, name="bank_a")
+                for e in range(2):
+                    product(im[:, e, :], w2, w2s, 2 * pair + e, xq[h][:], xq_s[:, h * HALF : (h + 1) * HALF])
+                square = squares[h][:, 2 * pair : 2 * pair + 2, :]
+                nc.scalar.activation(out=square, in_=im[:], func=ACT.Square)
+                inv_mg[h, pair] = sb([P, 2, HALF], F32, "inv_mg%d%d" % (h, pair))
+                nc.scalar.activation(out=inv_mg[h, pair][:], in_=square, func=ACT.Abs_reciprocal_sqrt, bias=quarter[:])
+
+        w1q = sb([P, H], U32, "w1q")
+        w1s = sb([P, H], U8, "w1s")
+        nc.vector.quantize_mx(out=w1q[:].bitcast(FP8X4), scales=w1s[:], in_=w1_bf[:].rearrange("p c j -> p (c j)"))
+        w3 = sb([P, N], I32, "w3")
+        w3s = sb([P, N], U8, "w3s")
+        deal(nc, w3[:], w3_raw[:])
+        deal(nc, w3s[:], w3s_raw[:])
+
+        y_words = sb([P, S], U32, "y_words")
+        y_scales = sb([P, S], U8, "y_scales")
+        out_rows = out_0.rearrange("(p t) n -> p t n", t=PACK)
+        out_words = words_of(out_1)
+        ratio = [sb([P, PACK, HALF], F32, "ratio0"), sb([P, PACK, HALF], F32, "inv_mg01")]
+        rest_on_scalar = [1,1,1,0]
+        cast_on_scalar = [1,1,1,0]
+        gather_width = [256,128]
+        rest = {}
+        first = 0
+        for c, width in enumerate(CHUNKS):
+            h, lo = divmod(first, HALF)
+            frames = slice(first, first + width)
+            gw = gather_width[h]
+            if first % gw == 0:
+                for t in range(PACK):
+                    looked_up = noise_sb[t][:].indirect(pr_sb[:, first // LIST_ROWS : (first + gw) // LIST_ROWS])
+                    nc.vector.tensor_tensor(
+                        out=ratio[h][:, t, lo : lo + gw], in0=looked_up, in1=inv_mg[h, t // 2][:, t % 2, lo : lo + gw], op=ALU.mult
+                    )
+            re = psum_b.tile([P, PACK, width], F32, name="bank_b")
+            for t in range(PACK):
+                product(re[:, t, :], w1q, w1s, t, xq[h][:, lo : lo + width], xq_s[:, frames])
+            rest = sb([P, width, PACK], F32, "rest%d" % c)
+            rest_view = rest[:].rearrange("p (b i) t -> p b t i", i=4)
+            ratio_view = ratio[h][:, :, lo : lo + width].rearrange("p t (b i) -> p b t i", i=4)
+            if rest_on_scalar[c]:
+                nc.scalar.activation(out=rest_view, in_=ratio_view, func=ACT.Identity, scale=-1.0, bias=one[:])
+            else:
+                nc.vector.tensor_scalar(
+                    out=rest_view, in0=ratio_view, scalar1=-1.0, scalar2=1.0, op0=ALU.mult, op1=ALU.add
+                )
+            z = sb([P, width, PACK], BF16, "z%d" % c)
+            nc.vector.scalar_tensor_tensor(
+                out=z[:], in0=rest[:], scalar=0.25, in1=re[:].rearrange("p t n -> p n t"), op0=ALU.max, op1=ALU.mult
+            )
+            zq = sb([P, width], U32, "zq%d" % c)
+            zs = sb([P, width], U8, "zs%d" % c)
+            nc.vector.quantize_mx(out=zq[:].bitcast(FP8X4), scales=zs[:], in_=z[:].rearrange("p n t -> p (n t)"))
+            y = psum_a.tile([P, PACK, width], F32, name="bank_a")
+            for t in range(PACK):
+                product(y[:, t, :], w3, w3s, t, zq[:], zs[:])
+            y_sb = sb([P, PACK, width], F32, "y_sb%d" % c)
+            y_bf = sb([P, width, PACK], BF16, "y_bf%d" % c)
+            nc.scalar.copy(out=y_sb[:], in_=y[:])
+            nc.sync.dma_start(out=out_rows[:, :, frames], in_=y_sb[:])
+            if cast_on_scalar[c]:
+                nc.scalar.copy(out=y_bf[:], in_=y[:].rearrange("p t n -> p n t"))
+            else:
+                nc.vector.tensor_copy(
+                    out=y_bf[:].rearrange("p (b i) t -> p b t i", i=4), in_=y_sb[:].rearrange("p t (b i) -> p b t i", i=4)
+                )
+            nc.vector.quantize_mx(
+                out=y_words[:, frames].bitcast(FP8X4), scales=y_scales[:, frames], in_=y_bf[:].rearrange("p n t -> p (n t)")
+            )
+            first = first + width
+            if first % HALF == 0:
+                both = slice(first - HALF, first)
+                nc.sync.dma_start(out=out_words[:, both], in_=y_words[:, both].bitcast(I32))
+        for q in range(4):
+            queue = nc.scalar if q % 2 == 0 else nc.sync
+            queue.dma_start(
+                out=out_2[0, 4 * q : 4 * q + 4, :].bitcast(I32), in_=y_scales[32 * q : 32 * q + 4, :].bitcast(I32)
+            )

@@ -139,21 +139,17 @@ def tile_picked_specsub_none_po_kernel(
         out_rows = out_0.rearrange("(p t) n -> p t n", t=PACK)
         out_words = words_of(out_1)
         ratio = [sb([P, PACK, HALF], F32, "ratio0"), sb([P, PACK, HALF], F32, "inv_mg01")]
-        rest_on_scalar = [1,1,1,0]
-        cast_on_scalar = [1,1,1,0]
-        gather_width = [256,128]
-        rest = {}
-        first = 0
+        rest_on_scalar = [1,1,1,1,1,1]
+        cast_on_scalar = [0,0,0,0,0,0]
+        for h in range(halves):
+            for t in range(PACK):
+                looked_up = noise_sb[t][:].indirect(pr_sb[:, h * cols : (h + 1) * cols])
+                nc.vector.tensor_tensor(out=ratio[h][:, t, :], in0=looked_up, in1=inv_mg[h, t // 2][:, t % 2, :], op=ALU.mult)
+        starts = [sum(CHUNKS[:c]) for c in range(len(CHUNKS))]
+        zq, zs = [], []
         for c, width in enumerate(CHUNKS):
-            h, lo = divmod(first, HALF)
-            frames = slice(first, first + width)
-            gw = gather_width[h]
-            if first % gw == 0:
-                for t in range(PACK):
-                    looked_up = noise_sb[t][:].indirect(pr_sb[:, first // LIST_ROWS : (first + gw) // LIST_ROWS])
-                    nc.vector.tensor_tensor(
-                        out=ratio[h][:, t, lo : lo + gw], in0=looked_up, in1=inv_mg[h, t // 2][:, t % 2, lo : lo + gw], op=ALU.mult
-                    )
+            h, lo = divmod(starts[c], HALF)
+            frames = slice(starts[c], starts[c] + width)
             re = psum_b.tile([P, PACK, width], F32, name="bank_b")
             for t in range(PACK):
                 product(re[:, t, :], w1q, w1s, t, xq[h][:, lo : lo + width], xq_s[:, frames])
@@ -170,12 +166,14 @@ def tile_picked_specsub_none_po_kernel(
             nc.vector.scalar_tensor_tensor(
                 out=z[:], in0=rest[:], scalar=0.25, in1=re[:].rearrange("p t n -> p n t"), op0=ALU.max, op1=ALU.mult
             )
-            zq = sb([P, width], U32, "zq%d" % c)
-            zs = sb([P, width], U8, "zs%d" % c)
-            nc.vector.quantize_mx(out=zq[:].bitcast(FP8X4), scales=zs[:], in_=z[:].rearrange("p n t -> p (n t)"))
+            zq.append(sb([P, width], U32, "zq%d" % c))
+            zs.append(sb([P, width], U8, "zs%d" % c))
+            nc.vector.quantize_mx(out=zq[c][:].bitcast(FP8X4), scales=zs[c][:], in_=z[:].rearrange("p n t -> p (n t)"))
+        for c, width in enumerate(CHUNKS):
+            frames = slice(starts[c], starts[c] + width)
             y = psum_a.tile([P, PACK, width], F32, name="bank_a")
             for t in range(PACK):
-                product(y[:, t, :], w3, w3s, t, zq[:], zs[:])
+                product(y[:, t, :], w3, w3s, t, zq[c][:], zs[c][:])
             y_sb = sb([P, PACK, width], F32, "y_sb%d" % c)
             y_bf = sb([P, width, PACK], BF16, "y_bf%d" % c)
             nc.scalar.copy(out=y_sb[:], in_=y[:])
@@ -189,9 +187,8 @@ def tile_picked_specsub_none_po_kernel(
             nc.vector.quantize_mx(
                 out=y_words[:, frames].bitcast(FP8X4), scales=y_scales[:, frames], in_=y_bf[:].rearrange("p n t -> p (n t)")
             )
-            first = first + width
-            if first % HALF == 0:
-                both = slice(first - HALF, first)
+            if frames.stop % HALF == 0:
+                both = slice(frames.stop - HALF, frames.stop)
                 nc.sync.dma_start(out=out_words[:, both], in_=y_words[:, both].bitcast(I32))
         for q in range(4):
             queue = nc.scalar if q % 2 == 0 else nc.sync

@@ -36,6 +36,10 @@ def deal(nc, dst, src):
     nc.vector.tensor_copy(out=dst.rearrange("p (t m) -> p m t", t=PACK), in_=src.rearrange("p (m t) -> p m t", t=PACK))
 
 
+def deal_bytes(nc, dst, src):
+    nc.gpsimd.tensor_copy(out=dst.rearrange("p (t m) -> p t m", t=PACK), in_=src.rearrange("p (m t) -> p t m", t=PACK))
+
+
 def tile_picked_specsub_none_po_kernel(
     tc, x_words, x_scales, w1, w2_words, w2_scales, noise, w3_words, w3_scales, offs, pr, out_0, out_1, out_2
 ):
@@ -83,9 +87,9 @@ def tile_picked_specsub_none_po_kernel(
         nc.sync.dma_start(out=w1_raw[1][:], in_=w1_rows[:, :, W1_SPLIT:H])
         nc.sync.dma_start(out=w3_raw[:], in_=words_of(w3_words))
         nc.sync.dma_start(out=pr_sb[:], in_=pr)
-        load_scale_rows(nc.sync, w3s_raw, w3_scales)
         for t in range(PACK):
             nc.sync.dma_start(out=noise_sb[t][:], in_=noise_rows[:, t, :])
+        load_scale_rows(nc.sync, w3s_raw, w3_scales)
 
         cols = HALF // LIST_ROWS
         xq_s = sb([P, S], U8, "xq_s")
@@ -121,18 +125,19 @@ def tile_picked_specsub_none_po_kernel(
                 im = psum_a.tile([P, 2, HALF], F32, name="bank_a")
                 for e in range(2):
                     product(im[:, e, :], w2, w2s, 2 * pair + e, xq[h][:], xq_s[:, h * HALF : (h + 1) * HALF])
-                square = squares[h][:, 2 * pair : 2 * pair + 2, :]
-                nc.scalar.activation(out=square, in_=im[:], func=ACT.Square)
                 inv_mg[h, pair] = sb([P, 2, HALF], F32, "inv_mg%d%d" % (h, pair))
-                nc.scalar.activation(out=inv_mg[h, pair][:], in_=square, func=ACT.Abs_reciprocal_sqrt, bias=quarter[:])
+                for e in range(2):
+                    nc.scalar.activation(out=squares[h][:, 2 * pair + e, :], in_=im[:, e, :], func=ACT.Square)
+                for e in range(2):
+                    nc.scalar.activation(
+                        out=inv_mg[h, pair][:, e, :], in_=squares[h][:, 2 * pair + e, :], func=ACT.Abs_reciprocal_sqrt, bias=quarter[:]
+                    )
 
         w1q = sb([P, H], U32, "w1q")
         w1s = sb([P, H], U8, "w1s")
         nc.vector.quantize_mx(out=w1q[:].bitcast(FP8X4), scales=w1s[:], in_=w1_bf[:].rearrange("p c j -> p (c j)"))
         w3 = sb([P, N], I32, "w3")
-        w3s = sb([P, N], U8, "w3s")
         deal(nc, w3[:], w3_raw[:])
-        deal(nc, w3s[:], w3s_raw[:])
 
         y_words = sb([P, S], U32, "y_words")
         y_scales = sb([P, S], U8, "y_scales")
@@ -145,6 +150,8 @@ def tile_picked_specsub_none_po_kernel(
             for t in range(PACK):
                 looked_up = noise_sb[t][:].indirect(pr_sb[:, h * cols : (h + 1) * cols])
                 nc.vector.tensor_tensor(out=ratio[h][:, t, :], in0=looked_up, in1=inv_mg[h, t // 2][:, t % 2, :], op=ALU.mult)
+        w3s = sb([P, N], U8, "inv_mg11")
+        deal_bytes(nc, w3s[:], w3s_raw[:])
         starts = [sum(CHUNKS[:c]) for c in range(len(CHUNKS))]
         zq, zs = [], []
         for c, width in enumerate(CHUNKS):

@@ -18,9 +18,8 @@ ACT = mybir.ActivationFunctionType
 P = 128
 PACK = 4
 HALF = 256
-CHUNKS = (128,128,128,128)
+CHUNK = 128
 LIST_ROWS = 16
-W1_SPLIT = 256
 
 
 def words_of(dram):
@@ -32,19 +31,20 @@ def load_scale_rows(queue, tile, dram):
         queue.dma_start(out=tile[32 * q : 32 * q + 4, :].bitcast(I32), in_=dram[0, 4 * q : 4 * q + 4, :].bitcast(I32))
 
 
-def deal(nc, dst, src):
-    nc.vector.tensor_copy(out=dst.rearrange("p (t m) -> p m t", t=PACK), in_=src.rearrange("p (m t) -> p m t", t=PACK))
+def deal(engine, dst, src, lo=0, hi=PACK):
+    engine.tensor_copy(
+        out=dst.rearrange("p (t m) -> p t m", t=PACK)[:, lo:hi], in_=src.rearrange("p (m t) -> p t m", t=PACK)[:, lo:hi]
+    )
 
 
-def deal_bytes(nc, dst, src):
-    nc.gpsimd.tensor_copy(out=dst.rearrange("p (t m) -> p t m", t=PACK), in_=src.rearrange("p (m t) -> p t m", t=PACK))
+def deal_words(engine, dst, src):
+    engine.tensor_copy(out=dst.rearrange("p (t m) -> p m t", t=PACK), in_=src.rearrange("p (m t) -> p m t", t=PACK))
 
 
 def tile_picked_specsub_none_po_kernel(
     tc, x_words, x_scales, w1, w2_words, w2_scales, noise, w3_words, w3_scales, offs, pr, out_0, out_1, out_2
 ):
     nc = tc.nc
-    halves = S // HALF
     with ExitStack() as ctx:
         lists = ctx.enter_context(tc.tile_pool(name="lists", bufs=1))
         keep = ctx.enter_context(tc.tile_pool(name="keep", bufs=1))
@@ -62,18 +62,18 @@ def tile_picked_specsub_none_po_kernel(
         w3_raw = sb([P, N], I32, "w3_raw")
         w2s_raw = sb([P, H], U8, "w2s_raw")
         w3s_raw = sb([P, N], U8, "w3s_raw")
-        w1_raw = [sb([P, PACK, W1_SPLIT], F32, "w1a"), sb([P, PACK, H - W1_SPLIT], F32, "w1b")]
+        w1_rows_sb = [sb([P, PACK * HALF], F32, "w1_raw%d" % a) for a in range(2)]
+        w1_raw = [rows[:].rearrange("p (j c) -> p j c", j=PACK) for rows in w1_rows_sb]
         noise_sb = [sb([P, U], F32, "noise%d" % t) for t in range(PACK)]
         quarter = sb([P, 1], F32, "quarter")
         one = sb([P, 1], F32, "one")
         warm = sb([P, 1], F32, "warm")
 
-        nc.vector.memset(xs_all[:, 0 : T // 2].bitcast(I32), 0)
-        nc.gpsimd.memset(xs_all[:, T // 2 : T].bitcast(I32), 0)
+        nc.gpsimd.memset(xs_all[:].bitcast(I32), 0)
+        nc.vector.memset(quarter[:], 0.25)
         nc.vector.memset(w2s_raw[:].bitcast(I32), 0)
         nc.vector.memset(w3s_raw[:].bitcast(I32), 0)
-        nc.gpsimd.memset(quarter[:], 0.25)
-        nc.gpsimd.memset(one[:], 1.0)
+        nc.vector.memset(one[:], 1.0)
         nc.scalar.activation(out=warm[:], in_=quarter[:], func=ACT.Abs_reciprocal_sqrt)
 
         noise_rows = noise.rearrange("(p t) u -> p t u", t=PACK)
@@ -83,23 +83,25 @@ def tile_picked_specsub_none_po_kernel(
         load_scale_rows(nc.sync, xs_all, x_scales)
         nc.sync.dma_start(out=x_all[:].bitcast(I32), in_=words_of(x_words))
         load_scale_rows(nc.sync, w2s_raw, w2_scales)
-        nc.sync.dma_start(out=w1_raw[0][:], in_=w1_rows[:, :, 0:W1_SPLIT])
-        nc.sync.dma_start(out=w1_raw[1][:], in_=w1_rows[:, :, W1_SPLIT:H])
-        nc.sync.dma_start(out=w3_raw[:], in_=words_of(w3_words))
-        nc.sync.dma_start(out=pr_sb[:], in_=pr)
+        nc.sync.dma_start(out=w1_raw[0], in_=w1_rows[:, :, 0:HALF])
         for t in range(PACK):
             nc.sync.dma_start(out=noise_sb[t][:], in_=noise_rows[:, t, :])
+            if t == 1:
+                nc.sync.dma_start(out=pr_sb[:], in_=pr)
+        nc.sync.dma_start(out=w1_raw[1], in_=w1_rows[:, :, HALF:H])
+        nc.sync.dma_start(out=w3_raw[:], in_=words_of(w3_words))
         load_scale_rows(nc.sync, w3s_raw, w3_scales)
 
         cols = HALF // LIST_ROWS
         xq_s = sb([P, S], U8, "xq_s")
-        xq = [sb([P, HALF], U32, "xq0"), sb([P, HALF], U32, "w2s_raw")]
+        xq = [sb([P, HALF], U32, "xq0"), sb([P, HALF], U32, "xq1")]
         w2 = sb([P, H], I32, "w2")
         w2s = sb([P, H], U8, "w2s")
         nc.vector.tensor_copy(out=xq_s[:], in_=xs_all[:].indirect(offs_sb[:]))
-        deal(nc, w2[:], w2_raw[:])
         nc.vector.tensor_copy(out=xq[0][:], in_=x_all[:].indirect(offs_sb[:, 0:cols]))
-        deal(nc, w2s[:], w2s_raw[:])
+        deal_words(nc.vector, w2[:], w2_raw[:])
+        deal(nc.gpsimd, w2s[:], w2s_raw[:], 0, 2)
+        deal(nc.gpsimd, w2s[:], w2s_raw[:], 2, PACK)
         nc.vector.tensor_copy(out=xq[1][:], in_=x_all[:].indirect(offs_sb[:, cols : 2 * cols]))
 
         def product(out, w, ws, t, rhs, rhs_scale):
@@ -113,84 +115,88 @@ def tile_picked_specsub_none_po_kernel(
                 stop=True,
             )
 
-        w1_bf = sb([P, H, PACK], BF16, "w1_bf")
-        w1_dealt = w1_bf[:].rearrange("p (t m) j -> p m j t", t=PACK)
-        nc.scalar.copy(out=w1_dealt[:, 0 : W1_SPLIT // PACK], in_=w1_raw[0][:].rearrange("p j (m t) -> p m j t", t=PACK))
-        nc.vector.tensor_copy(out=w1_dealt[:, W1_SPLIT // PACK :], in_=w1_raw[1][:].rearrange("p j (m t) -> p m j t", t=PACK))
-        squares = [sb([P, PACK, HALF], F32, "w1a"), sb([P, PACK, HALF], F32, "w1b")]
-
-        inv_mg = {}
-        for h in range(halves):
-            for pair in range(PACK // 2):
-                im = psum_a.tile([P, 2, HALF], F32, name="bank_a")
-                for e in range(2):
-                    product(im[:, e, :], w2, w2s, 2 * pair + e, xq[h][:], xq_s[:, h * HALF : (h + 1) * HALF])
-                inv_mg[h, pair] = sb([P, 2, HALF], F32, "inv_mg%d%d" % (h, pair))
-                for e in range(2):
-                    nc.scalar.activation(out=squares[h][:, 2 * pair + e, :], in_=im[:, e, :], func=ACT.Square)
-                for e in range(2):
-                    nc.scalar.activation(
-                        out=inv_mg[h, pair][:, e, :], in_=squares[h][:, 2 * pair + e, :], func=ACT.Abs_reciprocal_sqrt, bias=quarter[:]
-                    )
-
+        ratio = [sb([P, PACK, HALF], F32, "ratio%d" % h) for h in range(2)]
+        w1_flat = keep.tile([P, H * PACK], BF16, name="w1_bf", align_bytes=64)[:]
+        w1_bf = w1_flat.rearrange("p (t m j) -> p m j t", t=PACK, j=PACK)
         w1q = sb([P, H], U32, "w1q")
         w1s = sb([P, H], U8, "w1s")
-        nc.vector.quantize_mx(out=w1q[:].bitcast(FP8X4), scales=w1s[:], in_=w1_bf[:].rearrange("p c j -> p (c j)"))
+
+        def round_w1(copy, a, lo, hi):
+            copy(out=w1_bf[:, a * P // 2 + lo : a * P // 2 + hi], in_=w1_raw[a].rearrange("p j (m t) -> p m j t", t=PACK)[:, lo:hi])
+
+        round_w1(nc.vector.tensor_copy, 0, 0, P // 2)
+
+        pieces = [(2 * pair + e, h) for pair in range(2) for h in range(2) for e in range(2)]
+        square = [keep.tile([P, HALF], F32, name="square%d" % i, align_bytes=64)[:] for i in range(len(pieces) - 2)]
+        square = square + [w1_rows_sb[1][:, 2 * HALF : 3 * HALF], w1_rows_sb[1][:, 3 * HALF : 4 * HALF]]
+        inv_mg = [sb([P, HALF], F32, "inv_mg%d" % i) for i in range(len(pieces))]
+        for first in range(0, len(pieces), 2):
+            if first == len(pieces) - 2:
+                round_w1(nc.scalar.copy, 1, 0, P // 2)
+            for i in (first, first + 1):
+                t, h = pieces[i]
+                im = psum_a.tile([P, HALF], F32, name="bank_a")
+                product(im[:], w2, w2s, t, xq[h][:], xq_s[:, h * HALF : (h + 1) * HALF])
+                nc.scalar.activation(out=square[i], in_=im[:], func=ACT.Square)
+            for i in (first, first + 1):
+                nc.scalar.activation(out=inv_mg[i][:], in_=square[i], func=ACT.Abs_reciprocal_sqrt, bias=quarter[:])
+
+        def gather_noise(i):
+            t, h = pieces[i]
+            looked_up = noise_sb[t][:].indirect(pr_sb[:, h * cols : (h + 1) * cols])
+            nc.vector.tensor_tensor(out=ratio[h][:, t, :], in0=looked_up, in1=inv_mg[i][:], op=ALU.mult)
+
         w3 = sb([P, N], I32, "w3")
-        deal(nc, w3[:], w3_raw[:])
+        for i in range(len(pieces)):
+            if i == len(pieces) - 2:
+                deal_words(nc.vector, w3[:], w3_raw[:])
+                nc.vector.quantize_mx(out=w1q[:].bitcast(FP8X4), scales=w1s[:], in_=w1_flat)
+            gather_noise(i)
+        w3s = sb([P, N], U8, "inv_mg7")
+        deal(nc.gpsimd, w3s[:], w3s_raw[:])
+
+        chunks = S // CHUNK
+        rest_rows = [w1_rows_sb[1], sb([P, PACK * HALF], F32, "rest1")]
+        rest_half = [rows[:].rearrange("p (e n t) -> p e n t", e=2, t=PACK) for rows in rest_rows]
+        z = [sb([P, CHUNK, PACK], BF16, "z%d" % c) for c in range(chunks)]
+        zq = [sb([P, CHUNK], U32, "zq%d" % c) for c in range(chunks)]
+        zs = [sb([P, CHUNK], U8, "zs%d" % c) for c in range(chunks)]
+        for c in range(chunks + 1):
+            if c < chunks:
+                h, lo = divmod(c * CHUNK, HALF)
+                re = psum_b.tile([P, PACK, CHUNK], F32, name="bank_b")
+                for t in range(PACK):
+                    product(re[:, t, :], w1q, w1s, t, xq[h][:, lo : lo + CHUNK], xq_s[:, c * CHUNK : (c + 1) * CHUNK])
+                rest = rest_half[h][:, c % 2]
+                nc.scalar.activation(
+                    out=rest.rearrange("p (b i) t -> p b t i", i=4),
+                    in_=ratio[h][:, :, lo : lo + CHUNK].rearrange("p t (b i) -> p b t i", i=4),
+                    func=ACT.Identity,
+                    scale=-1.0,
+                    bias=one[:],
+                )
+                nc.vector.scalar_tensor_tensor(
+                    out=z[c][:], in0=rest, scalar=0.25, in1=re[:].rearrange("p t n -> p n t"), op0=ALU.max, op1=ALU.mult
+                )
+            if c > 0:
+                nc.vector.quantize_mx(out=zq[c - 1][:].bitcast(FP8X4), scales=zs[c - 1][:], in_=z[c - 1][:].rearrange("p n t -> p (n t)"))
 
         y_words = sb([P, S], U32, "y_words")
         y_scales = sb([P, S], U8, "y_scales")
         out_rows = out_0.rearrange("(p t) n -> p t n", t=PACK)
         out_words = words_of(out_1)
-        ratio = [sb([P, PACK, HALF], F32, "ratio0"), sb([P, PACK, HALF], F32, "inv_mg01")]
-        rest_on_scalar = [1,1,1,1,1,1]
-        cast_on_scalar = [0,0,0,0,0,0]
-        for h in range(halves):
-            for t in range(PACK):
-                looked_up = noise_sb[t][:].indirect(pr_sb[:, h * cols : (h + 1) * cols])
-                nc.vector.tensor_tensor(out=ratio[h][:, t, :], in0=looked_up, in1=inv_mg[h, t // 2][:, t % 2, :], op=ALU.mult)
-        w3s = sb([P, N], U8, "inv_mg11")
-        deal_bytes(nc, w3s[:], w3s_raw[:])
-        starts = [sum(CHUNKS[:c]) for c in range(len(CHUNKS))]
-        zq, zs = [], []
-        for c, width in enumerate(CHUNKS):
-            h, lo = divmod(starts[c], HALF)
-            frames = slice(starts[c], starts[c] + width)
-            re = psum_b.tile([P, PACK, width], F32, name="bank_b")
-            for t in range(PACK):
-                product(re[:, t, :], w1q, w1s, t, xq[h][:, lo : lo + width], xq_s[:, frames])
-            rest = sb([P, width, PACK], F32, "rest%d" % c)
-            rest_view = rest[:].rearrange("p (b i) t -> p b t i", i=4)
-            ratio_view = ratio[h][:, :, lo : lo + width].rearrange("p t (b i) -> p b t i", i=4)
-            if rest_on_scalar[c]:
-                nc.scalar.activation(out=rest_view, in_=ratio_view, func=ACT.Identity, scale=-1.0, bias=one[:])
-            else:
-                nc.vector.tensor_scalar(
-                    out=rest_view, in0=ratio_view, scalar1=-1.0, scalar2=1.0, op0=ALU.mult, op1=ALU.add
-                )
-            z = sb([P, width, PACK], BF16, "z%d" % c)
-            nc.vector.scalar_tensor_tensor(
-                out=z[:], in0=rest[:], scalar=0.25, in1=re[:].rearrange("p t n -> p n t"), op0=ALU.max, op1=ALU.mult
-            )
-            zq.append(sb([P, width], U32, "zq%d" % c))
-            zs.append(sb([P, width], U8, "zs%d" % c))
-            nc.vector.quantize_mx(out=zq[c][:].bitcast(FP8X4), scales=zs[c][:], in_=z[:].rearrange("p n t -> p (n t)"))
-        for c, width in enumerate(CHUNKS):
-            frames = slice(starts[c], starts[c] + width)
-            y = psum_a.tile([P, PACK, width], F32, name="bank_a")
+        for c in range(chunks):
+            frames = slice(c * CHUNK, (c + 1) * CHUNK)
+            y = psum_a.tile([P, PACK, CHUNK], F32, name="bank_a")
             for t in range(PACK):
                 product(y[:, t, :], w3, w3s, t, zq[c][:], zs[c][:])
-            y_sb = sb([P, PACK, width], F32, "y_sb%d" % c)
-            y_bf = sb([P, width, PACK], BF16, "y_bf%d" % c)
+            y_sb = sb([P, PACK, CHUNK], F32, "y_sb%d" % c)
+            y_bf = sb([P, CHUNK, PACK], BF16, "y_bf%d" % c)
             nc.scalar.copy(out=y_sb[:], in_=y[:])
             nc.sync.dma_start(out=out_rows[:, :, frames], in_=y_sb[:])
-            if cast_on_scalar[c]:
-                nc.scalar.copy(out=y_bf[:], in_=y[:].rearrange("p t n -> p n t"))
-            else:
-                nc.vector.tensor_copy(
-                    out=y_bf[:].rearrange("p (b i) t -> p b t i", i=4), in_=y_sb[:].rearrange("p t (b i) -> p b t i", i=4)
-                )
+            nc.vector.tensor_copy(
+                out=y_bf[:].rearrange("p (b i) t -> p b t i", i=4), in_=y_sb[:].rearrange("p t (b i) -> p b t i", i=4)
+            )
             nc.vector.quantize_mx(
                 out=y_words[:, frames].bitcast(FP8X4), scales=y_scales[:, frames], in_=y_bf[:].rearrange("p n t -> p (n t)")
             )

@@ -61,7 +61,6 @@ def tile_picked_specsub_none_po_kernel(
         w2_raw = sb([P, H], I32, "w2_raw")
         w3_raw = sb([P, N], I32, "w3_raw")
         w2s_raw = sb([P, H], U8, "w2s_raw")
-        w3s_raw = sb([P, N], U8, "w3s_raw")
         w1_rows_sb = [sb([P, PACK * HALF], F32, "w1_raw%d" % a) for a in range(2)]
         w1_raw = [rows[:].rearrange("p (j c) -> p j c", j=PACK) for rows in w1_rows_sb]
         noise_sb = [sb([P, U], F32, "noise%d" % t) for t in range(PACK)]
@@ -72,7 +71,6 @@ def tile_picked_specsub_none_po_kernel(
         nc.gpsimd.memset(xs_all[:].bitcast(I32), 0)
         nc.vector.memset(quarter[:], 0.25)
         nc.vector.memset(w2s_raw[:].bitcast(I32), 0)
-        nc.vector.memset(w3s_raw[:].bitcast(I32), 0)
         nc.vector.memset(one[:], 1.0)
         nc.scalar.activation(out=warm[:], in_=quarter[:], func=ACT.Abs_reciprocal_sqrt)
 
@@ -90,7 +88,6 @@ def tile_picked_specsub_none_po_kernel(
                 nc.sync.dma_start(out=pr_sb[:], in_=pr)
         nc.sync.dma_start(out=w1_raw[1], in_=w1_rows[:, :, HALF:H])
         nc.sync.dma_start(out=w3_raw[:], in_=words_of(w3_words))
-        load_scale_rows(nc.sync, w3s_raw, w3_scales)
 
         cols = HALF // LIST_ROWS
         xq_s = sb([P, S], U8, "xq_s")
@@ -102,6 +99,7 @@ def tile_picked_specsub_none_po_kernel(
         deal_words(nc.vector, w2[:], w2_raw[:])
         deal(nc.gpsimd, w2s[:], w2s_raw[:], 0, 2)
         deal(nc.gpsimd, w2s[:], w2s_raw[:], 2, PACK)
+        load_scale_rows(nc.gpsimd, w2s_raw, w3_scales)
         nc.vector.tensor_copy(out=xq[1][:], in_=x_all[:].indirect(offs_sb[:, cols : 2 * cols]))
 
         def product(out, w, ws, t, rhs, rhs_scale):
@@ -153,7 +151,7 @@ def tile_picked_specsub_none_po_kernel(
                 nc.vector.quantize_mx(out=w1q[:].bitcast(FP8X4), scales=w1s[:], in_=w1_flat)
             gather_noise(i)
         w3s = sb([P, N], U8, "inv_mg7")
-        deal(nc.gpsimd, w3s[:], w3s_raw[:])
+        deal(nc.gpsimd, w3s[:], w2s_raw[:])
 
         chunks = S // CHUNK
         rest_rows = [w1_rows_sb[1], sb([P, PACK * HALF], F32, "rest1")]
@@ -185,24 +183,34 @@ def tile_picked_specsub_none_po_kernel(
         y_scales = sb([P, S], U8, "y_scales")
         out_rows = out_0.rearrange("(p t) n -> p t n", t=PACK)
         out_words = words_of(out_1)
+        y_bf = sb([P, S, PACK], BF16, "z2")
+        def quantise_y(c):
+            frames = slice(c * CHUNK, (c + 1) * CHUNK)
+            nc.vector.quantize_mx(
+                out=y_words[:, frames].bitcast(FP8X4), scales=y_scales[:, frames], in_=y_bf[:, frames, :].rearrange("p n t -> p (n t)")
+            )
+            if c % 2 == 1:
+                both = slice(frames.stop - HALF, frames.stop)
+                nc.sync.dma_start(out=out_words[:, both], in_=y_words[:, both].bitcast(I32))
+
         for c in range(chunks):
             frames = slice(c * CHUNK, (c + 1) * CHUNK)
             y = psum_a.tile([P, PACK, CHUNK], F32, name="bank_a")
             for t in range(PACK):
                 product(y[:, t, :], w3, w3s, t, zq[c][:], zs[c][:])
             y_sb = sb([P, PACK, CHUNK], F32, "y_sb%d" % c)
-            y_bf = sb([P, CHUNK, PACK], BF16, "y_bf%d" % c)
+            rounded = y_bf[:, frames, :]
             nc.scalar.copy(out=y_sb[:], in_=y[:])
             nc.sync.dma_start(out=out_rows[:, :, frames], in_=y_sb[:])
-            nc.vector.tensor_copy(
-                out=y_bf[:].rearrange("p (b i) t -> p b t i", i=4), in_=y_sb[:].rearrange("p t (b i) -> p b t i", i=4)
-            )
-            nc.vector.quantize_mx(
-                out=y_words[:, frames].bitcast(FP8X4), scales=y_scales[:, frames], in_=y_bf[:].rearrange("p n t -> p (n t)")
-            )
-            if frames.stop % HALF == 0:
-                both = slice(frames.stop - HALF, frames.stop)
-                nc.sync.dma_start(out=out_words[:, both], in_=y_words[:, both].bitcast(I32))
+            if c == chunks - 1:
+                nc.scalar.copy(out=rounded, in_=y[:].rearrange("p t n -> p n t"))
+            else:
+                nc.vector.tensor_copy(
+                    out=rounded.rearrange("p (b i) t -> p b t i", i=4), in_=y_sb[:].rearrange("p t (b i) -> p b t i", i=4)
+                )
+            if c > 0:
+                quantise_y(c - 1)
+        quantise_y(chunks - 1)
         for q in range(4):
             queue = nc.scalar if q % 2 == 0 else nc.sync
             queue.dma_start(

@@ -20,6 +20,7 @@ PACK = 4
 HALF = 256
 CHUNK = 128
 LIST_ROWS = 16
+W1_FIRST = 320
 
 
 def words_of(dram):
@@ -61,8 +62,10 @@ def tile_picked_specsub_none_po_kernel(
         w2_raw = sb([P, H], I32, "w2_raw")
         w3_raw = sb([P, N], I32, "w3_raw")
         w2s_raw = sb([P, H], U8, "w2s_raw")
-        w1_rows_sb = [sb([P, PACK * HALF], F32, "w1_raw%d" % a) for a in range(2)]
-        w1_raw = [rows[:].rearrange("p (j c) -> p j c", j=PACK) for rows in w1_rows_sb]
+        w3s_raw = sb([P, N], U8, "w3s_raw")
+        w1_rows_sb = [sb([P, PACK * W1_FIRST], F32, "w1_raw0"), sb([P, PACK * HALF], F32, "w1_raw1")]
+        w1_cols = [slice(0, W1_FIRST), slice(W1_FIRST, H)]
+        w1_raw = [w1_rows_sb[a][:, 0 : PACK * (c.stop - c.start)].rearrange("p (j c) -> p j c", j=PACK) for a, c in enumerate(w1_cols)]
         noise_sb = [sb([P, U], F32, "noise%d" % t) for t in range(PACK)]
         quarter = sb([P, 1], F32, "quarter")
         one = sb([P, 1], F32, "one")
@@ -71,6 +74,7 @@ def tile_picked_specsub_none_po_kernel(
         nc.gpsimd.memset(xs_all[:].bitcast(I32), 0)
         nc.vector.memset(quarter[:], 0.25)
         nc.vector.memset(w2s_raw[:].bitcast(I32), 0)
+        nc.vector.memset(w3s_raw[:].bitcast(I32), 0)
         nc.vector.memset(one[:], 1.0)
         nc.scalar.activation(out=warm[:], in_=quarter[:], func=ACT.Abs_reciprocal_sqrt)
 
@@ -81,12 +85,14 @@ def tile_picked_specsub_none_po_kernel(
         load_scale_rows(nc.sync, xs_all, x_scales)
         nc.sync.dma_start(out=x_all[:].bitcast(I32), in_=words_of(x_words))
         load_scale_rows(nc.sync, w2s_raw, w2_scales)
-        nc.sync.dma_start(out=w1_raw[0], in_=w1_rows[:, :, 0:HALF])
+        nc.sync.dma_start(out=w1_raw[0], in_=w1_rows[:, :, w1_cols[0]])
         for t in range(PACK):
             nc.sync.dma_start(out=noise_sb[t][:], in_=noise_rows[:, t, :])
             if t == 1:
                 nc.sync.dma_start(out=pr_sb[:], in_=pr)
-        nc.sync.dma_start(out=w1_raw[1], in_=w1_rows[:, :, HALF:H])
+                load_scale_rows(nc.sync, w3s_raw, w3_scales)
+            if t == 2:
+                nc.sync.dma_start(out=w1_raw[1], in_=w1_rows[:, :, w1_cols[1]])
         nc.sync.dma_start(out=w3_raw[:], in_=words_of(w3_words))
 
         cols = HALF // LIST_ROWS
@@ -99,7 +105,6 @@ def tile_picked_specsub_none_po_kernel(
         deal_words(nc.vector, w2[:], w2_raw[:])
         deal(nc.gpsimd, w2s[:], w2s_raw[:], 0, 2)
         deal(nc.gpsimd, w2s[:], w2s_raw[:], 2, PACK)
-        load_scale_rows(nc.gpsimd, w2s_raw, w3_scales)
         nc.vector.tensor_copy(out=xq[1][:], in_=x_all[:].indirect(offs_sb[:, cols : 2 * cols]))
 
         def product(out, w, ws, t, rhs, rhs_scale):
@@ -119,18 +124,19 @@ def tile_picked_specsub_none_po_kernel(
         w1q = sb([P, H], U32, "w1q")
         w1s = sb([P, H], U8, "w1s")
 
-        def round_w1(copy, a, lo, hi):
-            copy(out=w1_bf[:, a * P // 2 + lo : a * P // 2 + hi], in_=w1_raw[a].rearrange("p j (m t) -> p m j t", t=PACK)[:, lo:hi])
+        def round_w1(copy, a):
+            groups = slice(w1_cols[a].start // PACK, w1_cols[a].stop // PACK)
+            copy(out=w1_bf[:, groups], in_=w1_raw[a].rearrange("p j (m t) -> p m j t", t=PACK))
 
-        round_w1(nc.vector.tensor_copy, 0, 0, P // 2)
+        round_w1(nc.vector.tensor_copy, 0)
 
         pieces = [(2 * pair + e, h) for pair in range(2) for h in range(2) for e in range(2)]
         square = [keep.tile([P, HALF], F32, name="square%d" % i, align_bytes=64)[:] for i in range(len(pieces) - 2)]
-        square = square + [w1_rows_sb[1][:, 2 * HALF : 3 * HALF], w1_rows_sb[1][:, 3 * HALF : 4 * HALF]]
+        square = square + [w1_rows_sb[1][:, HALF : 2 * HALF], w1_rows_sb[1][:, 2 * HALF : 3 * HALF]]
         inv_mg = [sb([P, HALF], F32, "inv_mg%d" % i) for i in range(len(pieces))]
         for first in range(0, len(pieces), 2):
             if first == len(pieces) - 2:
-                round_w1(nc.scalar.copy, 1, 0, P // 2)
+                round_w1(nc.scalar.copy, 1)
             for i in (first, first + 1):
                 t, h = pieces[i]
                 im = psum_a.tile([P, HALF], F32, name="bank_a")
@@ -151,7 +157,7 @@ def tile_picked_specsub_none_po_kernel(
                 nc.vector.quantize_mx(out=w1q[:].bitcast(FP8X4), scales=w1s[:], in_=w1_flat)
             gather_noise(i)
         w3s = sb([P, N], U8, "inv_mg7")
-        deal(nc.gpsimd, w3s[:], w2s_raw[:])
+        deal(nc.gpsimd, w3s[:], w3s_raw[:])
 
         chunks = S // CHUNK
         rest_rows = [w1_rows_sb[1], sb([P, PACK * HALF], F32, "rest1")]

@@ -28,8 +28,8 @@ def words_of(dram):
 
 
 def load_scale_rows(queue, tile, dram):
-    for q in range(4):
-        queue.dma_start(out=tile[32 * q : 32 * q + 4, :].bitcast(I32), in_=dram[0, 4 * q : 4 * q + 4, :].bitcast(I32))
+    for r in range(4):
+        queue.dma_start(out=tile[r:P:32, :].bitcast(I32), in_=dram[0, r:16:4, :].bitcast(I32))
 
 
 def deal(engine, dst, src, lo=0, hi=PACK):
@@ -217,8 +217,6 @@ def tile_picked_specsub_none_po_kernel(
             if c > 0:
                 quantise_y(c - 1)
         quantise_y(chunks - 1)
-        for q in range(4):
-            queue = nc.scalar if q % 2 == 0 else nc.sync
-            queue.dma_start(
-                out=out_2[0, 4 * q : 4 * q + 4, :].bitcast(I32), in_=y_scales[32 * q : 32 * q + 4, :].bitcast(I32)
-            )
+        for r in range(4):
+            queue = nc.scalar if r % 2 == 0 else nc.sync
+            queue.dma_start(out=out_2[0, r:16:4, :].bitcast(I32), in_=y_scales[r:P:32, :].bitcast(I32))

@@ -195,9 +195,7 @@ def tile_picked_specsub_none_po_kernel(
             nc.vector.quantize_mx(
                 out=y_words[:, frames].bitcast(FP8X4), scales=y_scales[:, frames], in_=y_bf[:, frames, :].rearrange("p n t -> p (n t)")
             )
-            if c % 2 == 1:
-                both = slice(frames.stop - HALF, frames.stop)
-                nc.sync.dma_start(out=out_words[:, both], in_=y_words[:, both].bitcast(I32))
+
 
         for c in range(chunks):
             frames = slice(c * CHUNK, (c + 1) * CHUNK)
@@ -217,6 +215,7 @@ def tile_picked_specsub_none_po_kernel(
             if c > 0:
                 quantise_y(c - 1)
         quantise_y(chunks - 1)
+        nc.sync.dma_start(out=out_words, in_=y_words[:].bitcast(I32))
         for r in range(4):
             queue = nc.scalar if r % 2 == 0 else nc.sync
             queue.dma_start(out=out_2[0, r:16:4, :].bitcast(I32), in_=y_scales[r:P:32, :].bitcast(I32))

@@ -156,7 +156,7 @@ def tile_picked_specsub_none_po_kernel(
                 deal_words(nc.vector, w3[:], w3_raw[:])
                 nc.vector.quantize_mx(out=w1q[:].bitcast(FP8X4), scales=w1s[:], in_=w1_flat)
             gather_noise(i)
-        w3s = sb([P, N], U8, "inv_mg7")
+        w3s = sb([P, N], U8, "inv_mg6")
         deal(nc.gpsimd, w3s[:], w3s_raw[:])
 
         chunks = S // CHUNK

from contextlib import ExitStack

import concourse.mybir as mybir

K, T, S, H, U, N = 512, 2048, 512, 512, 512, 512
FLOPS = 2 * (2 * K * H * S + H * N * S)

F32 = mybir.dt.float32
BF16 = mybir.dt.bfloat16
I32 = mybir.dt.int32
U32 = mybir.dt.uint32
U16 = mybir.dt.uint16
U8 = mybir.dt.uint8
FP8X4 = mybir.dt.float8_e4m3fn_x4
ALU = mybir.AluOpType
ACT = mybir.ActivationFunctionType

P = 128
PACK = 4
HALF = 256
CHUNK = 128
LIST_ROWS = 16
W1_FIRST = 320


def words_of(dram):
    return dram[0].rearrange("p n t -> p (n t)").bitcast(I32)


def load_scale_rows(queue, tile, dram):
    for r in range(4):
        queue.dma_start(out=tile[r:P:32, :].bitcast(I32), in_=dram[0, r:16:4, :].bitcast(I32))


def deal(engine, dst, src, lo=0, hi=PACK):
    engine.tensor_copy(
        out=dst.rearrange("p (t m) -> p t m", t=PACK)[:, lo:hi], in_=src.rearrange("p (m t) -> p t m", t=PACK)[:, lo:hi]
    )


def deal_words(engine, dst, src):
    engine.tensor_copy(out=dst.rearrange("p (t m) -> p m t", t=PACK), in_=src.rearrange("p (m t) -> p m t", t=PACK))


def tile_picked_specsub_none_po_kernel(
    tc, x_words, x_scales, w1, w2_words, w2_scales, noise, w3_words, w3_scales, offs, pr, out_0, out_1, out_2
):
    nc = tc.nc
    with ExitStack() as ctx:
        lists = ctx.enter_context(tc.tile_pool(name="lists", bufs=1))
        keep = ctx.enter_context(tc.tile_pool(name="keep", bufs=1))
        psum_a = ctx.enter_context(tc.psum_pool(name="psum_a", bufs=4))
        psum_b = ctx.enter_context(tc.psum_pool(name="psum_b", bufs=4))

        def sb(shape, dtype, name):
            return keep.tile(shape, dtype, name=name, align_bytes=64)

        offs_sb = lists.tile([P, S // LIST_ROWS], U16, name="offs_sb")
        pr_sb = lists.tile([P, S // LIST_ROWS], U16, name="pr_sb")
        x_all = sb([P, T], U32, "x_all")
        xs_all = sb([P, T], U8, "xs_all")
        w2_raw = sb([P, H], I32, "w2_raw")
        w3_raw = sb([P, N], I32, "w3_raw")
        w2s_raw = sb([P, H], U8, "w2s_raw")
        w3s_raw = sb([P, N], U8, "w3s_raw")
        w1_rows_sb = [sb([P, PACK * W1_FIRST], F32, "w1_raw0"), sb([P, PACK * HALF], F32, "w1_raw1")]
        w1_cols = [slice(0, W1_FIRST), slice(W1_FIRST, H)]
        w1_raw = [w1_rows_sb[a][:, 0 : PACK * (c.stop - c.start)].rearrange("p (j c) -> p j c", j=PACK) for a, c in enumerate(w1_cols)]
        noise_sb = [sb([P, U], F32, "noise%d" % t) for t in range(PACK)]
        quarter = sb([P, 1], F32, "quarter")
        one = sb([P, 1], F32, "one")
        warm = sb([P, 1], F32, "warm")

        nc.gpsimd.memset(xs_all[:].bitcast(I32), 0)
        nc.vector.memset(quarter[:], 0.25)
        nc.vector.memset(w2s_raw[:].bitcast(I32), 0)
        nc.vector.memset(w3s_raw[:].bitcast(I32), 0)
        nc.vector.memset(one[:], 1.0)
        nc.scalar.activation(out=warm[:], in_=quarter[:], func=ACT.Abs_reciprocal_sqrt)

        noise_rows = noise.rearrange("(p t) u -> p t u", t=PACK)
        w1_rows = w1.rearrange("(p j) c -> p j c", j=PACK)
        nc.sync.dma_start(out=offs_sb[:], in_=offs)
        nc.sync.dma_start(out=w2_raw[:], in_=words_of(w2_words))
        load_scale_rows(nc.sync, xs_all, x_scales)
        nc.sync.dma_start(out=x_all[:].bitcast(I32), in_=words_of(x_words))
        load_scale_rows(nc.sync, w2s_raw, w2_scales)
        nc.sync.dma_start(out=w1_raw[0], in_=w1_rows[:, :, w1_cols[0]])
        for t in range(PACK):
            nc.sync.dma_start(out=noise_sb[t][:], in_=noise_rows[:, t, :])
            if t == 1:
                nc.sync.dma_start(out=pr_sb[:], in_=pr)
                load_scale_rows(nc.sync, w3s_raw, w3_scales)
            if t == 2:
                nc.sync.dma_start(out=w1_raw[1], in_=w1_rows[:, :, w1_cols[1]])
        nc.sync.dma_start(out=w3_raw[:], in_=words_of(w3_words))

        cols = HALF // LIST_ROWS
        xq_s = sb([P, S], U8, "xq_s")
        xq = [sb([P, HALF], U32, "xq0"), sb([P, HALF], U32, "xq1")]
        w2 = sb([P, H], I32, "w2")
        w2s = sb([P, H], U8, "w2s")
        nc.vector.tensor_copy(out=xq_s[:], in_=xs_all[:].indirect(offs_sb[:]))
        nc.vector.tensor_copy(out=xq[0][:], in_=x_all[:].indirect(offs_sb[:, 0:cols]))
        deal_words(nc.vector, w2[:], w2_raw[:])
        deal(nc.gpsimd, w2s[:], w2s_raw[:], 0, 2)
        deal(nc.gpsimd, w2s[:], w2s_raw[:], 2, PACK)
        nc.vector.tensor_copy(out=xq[1][:], in_=x_all[:].indirect(offs_sb[:, cols : 2 * cols]))

        def product(out, w, ws, t, rhs, rhs_scale):
            nc.tensor.matmul_mx(
                out=out,
                lhsT=w[:, t * P : (t + 1) * P].bitcast(FP8X4),
                lhsT_scale=ws[:, t * P : (t + 1) * P],
                rhs=rhs.bitcast(FP8X4),
                rhs_scale=rhs_scale,
                start=True,
                stop=True,
            )

        ratio = [sb([P, PACK, HALF], F32, "ratio%d" % h) for h in range(2)]
        w1_flat = keep.tile([P, H * PACK], BF16, name="w1_bf", align_bytes=64)[:]
        w1_bf = w1_flat.rearrange("p (t m j) -> p m j t", t=PACK, j=PACK)
        w1q = sb([P, H], U32, "w1q")
        w1s = sb([P, H], U8, "w1s")

        def round_w1(copy, a):
            groups = slice(w1_cols[a].start // PACK, w1_cols[a].stop // PACK)
            copy(out=w1_bf[:, groups], in_=w1_raw[a].rearrange("p j (m t) -> p m j t", t=PACK))

        round_w1(nc.vector.tensor_copy, 0)

        pieces = [(2 * pair + e, h) for pair in range(2) for h in range(2) for e in range(2)]
        square = [keep.tile([P, HALF], F32, name="square%d" % i, align_bytes=64)[:] for i in range(len(pieces) - 2)]
        square = square + [w1_rows_sb[1][:, HALF : 2 * HALF], w1_rows_sb[1][:, 2 * HALF : 3 * HALF]]
        inv_mg = [sb([P, HALF], F32, "inv_mg%d" % i) for i in range(len(pieces))]
        for first in range(0, len(pieces), 2):
            if first == len(pieces) - 2:
                round_w1(nc.scalar.copy, 1)
            for i in (first, first + 1):
                t, h = pieces[i]
                im = psum_a.tile([P, HALF], F32, name="bank_a")
                product(im[:], w2, w2s, t, xq[h][:], xq_s[:, h * HALF : (h + 1) * HALF])
                nc.scalar.activation(out=square[i], in_=im[:], func=ACT.Square)
            for i in (first, first + 1):
                nc.scalar.activation(out=inv_mg[i][:], in_=square[i], func=ACT.Abs_reciprocal_sqrt, bias=quarter[:])

        def gather_noise(i):
            t, h = pieces[i]
            looked_up = noise_sb[t][:].indirect(pr_sb[:, h * cols : (h + 1) * cols])
            nc.vector.tensor_tensor(out=ratio[h][:, t, :], in0=looked_up, in1=inv_mg[i][:], op=ALU.mult)

        w3 = sb([P, N], I32, "w3")
        for i in range(len(pieces)):
            if i == len(pieces) - 2:
                deal_words(nc.vector, w3[:], w3_raw[:])
                nc.vector.quantize_mx(out=w1q[:].bitcast(FP8X4), scales=w1s[:], in_=w1_flat)
            gather_noise(i)
        w3s = sb([P, N], U8, "inv_mg6")
        deal(nc.gpsimd, w3s[:], w3s_raw[:])

        chunks = S // CHUNK
        rest_rows = [w1_rows_sb[1], sb([P, PACK * HALF], F32, "rest1")]
        rest_half = [rows[:].rearrange("p (e n t) -> p e n t", e=2, t=PACK) for rows in rest_rows]
        z = [sb([P, CHUNK, PACK], BF16, "z%d" % c) for c in range(chunks)]
        zq = [sb([P, CHUNK], U32, "zq%d" % c) for c in range(chunks)]
        zs = [sb([P, CHUNK], U8, "zs%d" % c) for c in range(chunks)]
        for c in range(chunks + 1):
            if c < chunks:
                h, lo = divmod(c * CHUNK, HALF)
                re = psum_b.tile([P, PACK, CHUNK], F32, name="bank_b")
                for t in range(PACK):
                    product(re[:, t, :], w1q, w1s, t, xq[h][:, lo : lo + CHUNK], xq_s[:, c * CHUNK : (c + 1) * CHUNK])
                rest = rest_half[h][:, c % 2]
                nc.scalar.activation(
                    out=rest.rearrange("p (b i) t -> p b t i", i=4),
                    in_=ratio[h][:, :, lo : lo + CHUNK].rearrange("p t (b i) -> p b t i", i=4),
                    func=ACT.Identity,
                    scale=-1.0,
                    bias=one[:],
                )
                nc.vector.scalar_tensor_tensor(
                    out=z[c][:], in0=rest, scalar=0.25, in1=re[:].rearrange("p t n -> p n t"), op0=ALU.max, op1=ALU.mult
                )
            if c > 0:
                nc.vector.quantize_mx(out=zq[c - 1][:].bitcast(FP8X4), scales=zs[c - 1][:], in_=z[c - 1][:].rearrange("p n t -> p (n t)"))

        y_words = sb([P, S], U32, "y_words")
        y_scales = sb([P, S], U8, "y_scales")
        out_rows = out_0.rearrange("(p t) n -> p t n", t=PACK)
        out_words = words_of(out_1)
        y_bf = sb([P, S, PACK], BF16, "z2")
        def quantise_y(c):
            frames = slice(c * CHUNK, (c + 1) * CHUNK)
            nc.vector.quantize_mx(
                out=y_words[:, frames].bitcast(FP8X4), scales=y_scales[:, frames], in_=y_bf[:, frames, :].rearrange("p n t -> p (n t)")
            )


        for c in range(chunks):
            frames = slice(c * CHUNK, (c + 1) * CHUNK)
            y = psum_a.tile([P, PACK, CHUNK], F32, name="bank_a")
            for t in range(PACK):
                product(y[:, t, :], w3, w3s, t, zq[c][:], zs[c][:])
            y_sb = sb([P, PACK, CHUNK], F32, "y_sb%d" % c)
            rounded = y_bf[:, frames, :]
            nc.scalar.copy(out=y_sb[:], in_=y[:])
            nc.sync.dma_start(out=out_rows[:, :, frames], in_=y_sb[:])
            if c == chunks - 1:
                nc.scalar.copy(out=rounded, in_=y[:].rearrange("p t n -> p n t"))
            else:
                nc.vector.tensor_copy(
                    out=rounded.rearrange("p (b i) t -> p b t i", i=4), in_=y_sb[:].rearrange("p t (b i) -> p b t i", i=4)
                )
            if c > 0:
                quantise_y(c - 1)
        quantise_y(chunks - 1)
        nc.sync.dma_start(out=out_words, in_=y_words[:].bitcast(I32))
        for r in range(4):
            queue = nc.scalar if r % 2 == 0 else nc.sync
            queue.dma_start(out=out_2[0, r:16:4, :].bitcast(I32), in_=y_scales[r:P:32, :].bitcast(I32))
